import numpy as np
import ml_dtypes


def mxq(x, axis, fmt="e4m3"):
    dtype, down = {"e4m3": (ml_dtypes.float8_e4m3fn, 7), "e5m2": (ml_dtypes.float8_e5m2, 14)}[fmt]
    v = np.moveaxis(np.asarray(x, np.float32).astype(ml_dtypes.bfloat16).astype(np.float64), axis, -1)
    blocks = v.reshape(v.shape[:-1] + (-1, 32))
    amax = np.abs(blocks).max(-1, keepdims=True)
    byte = np.maximum(np.where(amax > 0, np.frexp(amax)[1] - 1 + 127, 0) - down, 1)
    scale = np.exp2(byte - 127.0)
    codes = (blocks / scale).astype(np.float32).astype(dtype).astype(np.float64)
    return np.moveaxis((codes * scale).reshape(v.shape), -1, axis)


WIDE = False


def mx_kscale(k):
    if not WIDE:
        return np.ones(k)
    levels = np.array([10, -10, 5, -5, 0])
    if k % 512:
        return np.exp2(np.random.permutation(np.resize(levels, k // 32))).repeat(32)
    a = np.empty((k // 512, 16))
    for p in range(k // 512):
        a[p, :8] = np.random.permutation(np.resize(levels, 8))
        for g in range(8):
            far = levels[np.abs(levels - a[p, g]) >= 10]
            a[p, g + 8] = far[np.random.randint(len(far))]
    return np.exp2(a.ravel()).repeat(32)


def f64(x):
    return np.asarray(x).astype(np.float64)


def striped(idx):
    return np.tile(np.asarray(idx).reshape(-1, 16).T, (8, 1)).astype(np.uint16)


def unstriped(offs):
    return offs[:16].T.reshape(-1).astype(np.int64)


E2M1 = np.array([0.0, 0.5, 1.0, 1.5, 2.0, 3.0, 4.0, 6.0, -0.0, -0.5, -1.0, -1.5, -2.0, -3.0, -4.0, -6.0])


def pack_weight(w, fmt):
    k, n = w.shape
    w = f64(np.asarray(w, np.float32).astype(ml_dtypes.bfloat16)).reshape(k // 32, 32, n)
    amax = np.abs(w).max(1)
    if fmt == "e4m3":
        byte = np.frexp(amax)[1] - 1 + 127 - 7
    else:
        mant, ex = np.frexp(amax / 6.0)
        byte = np.where(mant > 0.5, ex, ex - 1) + 127
    byte = np.clip(np.where(amax > 0, byte, 1), 1, 254)
    scaled = (w * np.exp2(127.0 - byte)[:, None, :]).reshape(k, n).astype(np.float32)
    by_word = np.ascontiguousarray(scaled.reshape(k // 512, 128, 4, n).transpose(0, 1, 3, 2))
    if fmt == "e4m3":
        words = by_word.astype(ml_dtypes.float8_e4m3fn).view(np.uint8)
    else:
        c = by_word.astype(ml_dtypes.float4_e2m1fn).view(np.uint8) & 0xF
        words = (c[..., 0::2] | (c[..., 1::2] << 4)).reshape(k // 512, 128, 2 * n)
    return np.ascontiguousarray(words), np.ascontiguousarray(byte.astype(np.uint8).reshape(k // 512, 16, n))


def unpack_weight(words, scales, fmt):
    g, _, n = scales.shape
    words = np.ascontiguousarray(words).reshape(g, 128, n, -1)
    if fmt == "e4m3":
        vals = words.view(ml_dtypes.float8_e4m3fn).astype(np.float64)
    else:
        nib = np.empty((g, 128, n, 4), np.uint8)
        nib[..., 0::2] = words & 0xF
        nib[..., 1::2] = words >> 4
        vals = E2M1[nib]
    vals = vals * np.repeat(np.exp2(scales.astype(np.float64) - 127.0), 8, axis=1)[..., None]
    return vals.transpose(0, 1, 3, 2).reshape(g * 512, n)


def bf(x):
    return np.asarray(x, np.float32).astype(ml_dtypes.bfloat16)


def planes(Y):
    r, m = Y.shape
    b = f64(bf(Y)).reshape(r // 32, 32, m)
    amax = np.abs(b).max(1)
    byte = np.clip(np.where(amax > 0, np.frexp(amax)[1] - 1 + 127 - 7, 1), 1, 254)
    codes = (b * np.exp2(127.0 - byte)[:, None, :]).reshape(r, m).astype(np.float32).astype(ml_dtypes.float8_e4m3fn).view(np.uint8)
    words = codes.reshape(r // 512, 128, 4, m).transpose(0, 1, 3, 2)
    return np.ascontiguousarray(words), np.ascontiguousarray(byte.astype(np.uint8).reshape(r // 512, 16, m))


K, T, J, L, N = 1024, 2048, 512, 512, 512


def setup_inputs():
    n = np.random.standard_normal
    idx = np.random.permutation(T)[:J]
    fk = mx_kscale(K)
    fl = mx_kscale(L)
    wp = pack_weight(n((K, N)) * 1 / np.sqrt(K) * fk[:, None], "e2m1")
    cxp = pack_weight(n((L, J)) / fl[:, None], "e4m3")
    wcp = pack_weight(n((L, N)) * 1 / np.sqrt(L) * fl[:, None], "e2m1")
    return {
        "xt": (n((K, T)) / fk[:, None]).astype(np.float32),
        "w_words": wp[0],
        "w_scales": wp[1],
        "cx_words": cxp[0],
        "cx_scales": cxp[1],
        "wc_words": wcp[0],
        "wc_scales": wcp[1],
        "ta": (np.random.uniform(0.5, 2.0, (N, 1))).astype(np.float32),
        "tb": (np.random.uniform(-1.0, 1.0, (N, 1))).astype(np.float32),
        "td": (np.random.uniform(-0.5, 0.5, (N, 1))).astype(np.float32),
        "offs": striped(idx),
    }


def reference(xt, w_words, w_scales, cx_words, cx_scales, wc_words, wc_scales, ta, tb, td, offs):
    idx = unstriped(offs)
    wu = unpack_weight(w_words, w_scales, "e2m1")
    cxu = unpack_weight(cx_words, cx_scales, "e4m3")
    wcu = unpack_weight(wc_words, wc_scales, "e2m1")
    xtidxq = mxq(f64(xt)[:, idx], 0, "e4m3")
    z = wu.T @ xtidxq
    za = np.pad(z, ((0, 0), (1, 0)))[:, :J]
    zb = np.pad(z, ((0, 0), (2, 0)))[:, :J]
    s = wcu.T @ cxu
    y = f64(ta) * z + f64(tb) * za + f64(td) * zb + s
    words, scales = planes(y)
    return y, words, scales

@@ -1,0 +1,183 @@
+from contextlib import ExitStack
+
+import concourse.mybir as mybir
+
+K, T, J, L, N = 1024, 2048, 512, 512, 512
+FLOPS = 2 * K * N * J + 2 * L * N * J
+
+F32 = mybir.dt.float32
+BF16 = mybir.dt.bfloat16
+I32 = mybir.dt.int32
+U32 = mybir.dt.uint32
+U16 = mybir.dt.uint16
+U8 = mybir.dt.uint8
+FP8X4 = mybir.dt.float8_e4m3fn_x4
+FP4X4 = mybir.dt.float4_e2m1fn_x4
+MULT = mybir.AluOpType.mult
+ADD = mybir.AluOpType.add
+
+P = 128
+PACK = 4
+PASSES = K // (P * PACK)
+HALF = J // 2
+NMM = 128
+QUARTER = J // 4
+VEC_COLS = 80
+
+
+def tile_list_lagged_taps_pl_kernel(tc, xt, w_words, w_scales, cx_words, cx_scales, wc_words, wc_scales, ta, tb, td, offs, out_0, out_1, out_2):
+    nc = tc.nc
+    with ExitStack() as ctx:
+        sb = ctx.enter_context(tc.tile_pool(name="sb", bufs=1))
+        ps = ctx.enter_context(tc.psum_pool(name="ps", bufs=1))
+
+        offsets = sb.tile([P, J // 16], U16, name="offsets")
+        planes = [sb.tile([P, T], F32, name=f"plane{i}") for i in range(PASSES * PACK)]
+        xt_planes = xt.rearrange("(g p t) c -> g t p c", p=P, t=PACK)
+
+        w_raw = sb.tile([P, PASSES, N], U16, name="w_raw")
+        wc_raw = sb.tile([P, N], U16, name="wc_raw")
+        cx_codes = sb.tile([P, J], U32, name="cx_codes", align_bytes=64)
+        ws_raw = sb.tile([P, PASSES, N], U8, name="ws_raw")
+        wcs_raw = sb.tile([P, N], U8, name="wcs_raw")
+        cx_plane = sb.tile([P, J], U8, name="cx_plane", align_bytes=64)
+        taps = [sb.tile([P, PACK], F32, name=f"tap{i}") for i in range(3)]
+
+        nc.gpsimd.memset(ws_raw[:].rearrange("p g n -> p (g n)").bitcast(I32), 0)
+        nc.gpsimd.memset(wcs_raw[:].bitcast(I32), 0)
+        nc.gpsimd.memset(cx_plane[:].bitcast(I32), 0)
+
+        def load_plane(i):
+            nc.sync.dma_start(out=planes[i][:], in_=xt_planes[i // PACK, i % PACK])
+
+        def load_scales(tile, scales, quadrants):
+            for q in quadrants:
+                nc.sync.dma_start(out=tile[32 * q : 32 * q + 4].bitcast(I32), in_=scales[4 * q : 4 * q + 4].bitcast(I32))
+
+        nc.sync.dma_start(offsets[:], offs)
+        for tap_tile, tap in zip(taps, (ta, tb, td)):
+            nc.sync.dma_start(out=tap_tile[:], in_=tap.rearrange("(p t) o -> p (t o)", t=PACK))
+        nc.sync.dma_start(out=wc_raw[:].bitcast(I32), in_=wc_words[0].bitcast(I32))
+        nc.sync.dma_start(out=w_raw[:].bitcast(I32), in_=w_words.rearrange("g p b -> p g b").bitcast(I32))
+        load_plane(0)
+        scale_loads = [(ws_raw, w_scales.rearrange("g r n -> r g n")), (wcs_raw, wc_scales[0]), (cx_plane, cx_scales[0])]
+        for i in range(1, 7):
+            load_plane(i)
+            tile, scales = scale_loads[(i - 1) // 2]
+            load_scales(tile, scales, (0, 1) if i % 2 else (2, 3))
+        load_plane(7)
+        nc.sync.dma_start(out=cx_codes[:].bitcast(I32), in_=cx_words[0].rearrange("p c r -> p (c r)").bitcast(I32))
+
+        w_codes = sb.tile([P, PASSES, PACK, P], U16, name="w_codes", align_bytes=64)
+        wc_codes = sb.tile([P, PACK, P], U16, name="wc_codes", align_bytes=64)
+        w_plane = sb.tile([P, PASSES, PACK, P], U8, name="w_plane", align_bytes=64)
+        wc_plane = sb.tile([P, PACK, P], U8, name="wc_plane", align_bytes=64)
+
+        picked0 = sb.tile([P, PACK, J], BF16, name="picked0")
+        woven = [sb.tile([P, J, PACK], BF16, name=f"woven{g}", align_bytes=64) for g in range(PASSES)]
+        x_codes = [sb.tile([P, J], U32, name=f"x_codes{g}", align_bytes=64) for g in range(PASSES)]
+        x_plane = [sb.tile([P, J], U8, name=f"x_plane{g}", align_bytes=64) for g in range(PASSES)]
+
+        def gather0(t):
+            nc.vector.tensor_copy(picked0[:, t, :], planes[t][:].indirect(offsets[:]))
+
+        nc.vector.tensor_copy(wc_codes[:], wc_raw[:].rearrange("p (m t) -> p t m", t=PACK))
+        nc.vector.tensor_copy(w_codes[:], w_raw[:].rearrange("p g (m t) -> p g t m", t=PACK))
+        gather0(0)
+        gather0(1)
+        for g in range(PASSES):
+            nc.vector.tensor_copy(w_plane[:, g], ws_raw[:, g].rearrange("p (m t) -> p t m", t=PACK))
+        gather0(2)
+        gather0(3)
+        nc.vector.tensor_copy(wc_plane[:], wcs_raw[:].rearrange("p (m t) -> p t m", t=PACK))
+        nc.scalar.copy(woven[0][:].rearrange("p (c i) t -> p c t i", i=4), picked0[:].rearrange("p t (c i) -> p c t i", i=4))
+
+        acc = sb.tile([P, PACK, J], F32, name="acc")
+
+        def context_rows(t):
+            s_bank = ps.tile([P, J], F32, name=f"s_bank{t}")
+            nc.tensor.matmul_mx(out=s_bank[:], lhsT=wc_codes[:, t, :].bitcast(FP4X4), lhsT_scale=wc_plane[:, t, :], rhs=cx_codes[:].bitcast(FP8X4), rhs_scale=cx_plane[:], start=True, stop=True)
+            nc.scalar.copy(acc[:, t, :], s_bank[:])
+
+        def quantize_x(g, j0, width):
+            nc.vector.quantize_mx(out=x_codes[g][:, j0 : j0 + width].bitcast(FP8X4), scales=x_plane[g][:, j0 : j0 + width], in_=woven[g][:, j0 : j0 + width, :].rearrange("p c t -> p (c t)"))
+
+        z_banks = [[ps.tile([P, 2, HALF], F32, name=f"z_bank{h}{u}") for u in range(2)] for h in range(2)]
+
+        def z_pass(g, h, u):
+            for e in range(2):
+                for c in range(HALF // NMM):
+                    j0 = h * HALF + c * NMM
+                    nc.tensor.matmul_mx(
+                        out=z_banks[h][u][:, e, c * NMM : (c + 1) * NMM],
+                        lhsT=w_codes[:, g, 2 * u + e, :].bitcast(FP4X4),
+                        lhsT_scale=w_plane[:, g, 2 * u + e, :],
+                        rhs=x_codes[g][:, j0 : j0 + NMM].bitcast(FP8X4),
+                        rhs_scale=x_plane[g][:, j0 : j0 + NMM],
+                        start=(g == 0 and e == 0 and c == 0),
+                        stop=(g == PASSES - 1 and e == 1 and c == HALF // NMM - 1),
+                    )
+
+        nc.vector.tensor_copy(woven[1][:, :, 0], planes[PACK][:].indirect(offsets[:]))
+        quantize_x(0, 0, J)
+        for h in range(2):
+            for u in range(2):
+                z_pass(0, h, u)
+        for t in range(1, PACK - 1):
+            nc.vector.tensor_copy(woven[1][:, :, t], planes[PACK + t][:].indirect(offsets[:]))
+        for h in range(2):
+            j0 = h * HALF
+            nc.vector.tensor_copy(woven[1][:, j0 : j0 + HALF, PACK - 1], planes[2 * PACK - 1][:].indirect(offsets[:, j0 // 16 : (j0 + HALF) // 16]))
+            quantize_x(1, j0, HALF)
+
+        for u in range(2):
+            context_rows(2 * u)
+            context_rows(2 * u + 1)
+            z_pass(1, 0, u)
+        for u in range(2):
+            z_pass(1, 1, u)
+
+        y_woven = sb.tile([P, J, PACK], BF16, name="y_woven", align_bytes=64)
+        y_codes = sb.tile([P, J], U32, name="y_codes", align_bytes=64)
+        y_plane = sb.tile([P, J], U8, name="y_plane", align_bytes=64)
+        y_rows = out_0.rearrange("(p t) j -> p t j", t=PACK)
+        y_words = out_1[0].rearrange("p c r -> p (c r)").bitcast(I32)
+
+        def weave_y(engine_copy, j0, j1):
+            engine_copy(y_woven[:, j0:j1, :].rearrange("p (c i) t -> p c t i", i=4), acc[:, :, j0:j1].rearrange("p t (c i) -> p c t i", i=4))
+
+        def quantize_y(j0, width):
+            nc.vector.quantize_mx(out=y_codes[:, j0 : j0 + width].bitcast(FP8X4), scales=y_plane[:, j0 : j0 + width], in_=y_woven[:, j0 : j0 + width, :].rearrange("p c t -> p (c t)"))
+
+        def add_taps(h, u, c0, c1):
+            for lag in (2, 1, 0):
+                first = h * HALF + c0 + lag
+                width = min(c1 - c0, J - first)
+                for e in range(2):
+                    t = 2 * u + e
+                    cols = acc[:, t, first : first + width]
+                    nc.vector.scalar_tensor_tensor(cols, z_banks[h][u][:, e, c0 : c0 + width], taps[lag][:, t : t + 1], cols, MULT, ADD)
+
+        def store_y(h, u):
+            nc.sync.dma_start(out=y_rows[:, 2 * u : 2 * u + 2, h * HALF : (h + 1) * HALF], in_=acc[:, 2 * u : 2 * u + 2, h * HALF : (h + 1) * HALF])
+
+        for u in range(2):
+            add_taps(0, u, 0, HALF)
+            store_y(0, u)
+        weave_y(nc.scalar.copy, 0, HALF)
+        add_taps(1, 0, 0, HALF)
+        store_y(1, 0)
+        quantize_y(0, HALF)
+        nc.sync.dma_start(out=y_words[:, 0:HALF], in_=y_codes[:, 0:HALF].bitcast(I32))
+        add_taps(1, 1, 0, QUARTER)
+        weave_y(nc.scalar.copy, HALF, HALF + QUARTER)
+        add_taps(1, 1, QUARTER, HALF)
+        store_y(1, 1)
+        weave_y(nc.vector.tensor_copy, HALF + QUARTER, HALF + QUARTER + VEC_COLS)
+        weave_y(nc.scalar.copy, HALF + QUARTER + VEC_COLS, J)
+        quantize_y(HALF, QUARTER)
+        quantize_y(HALF + QUARTER, QUARTER)
+        nc.sync.dma_start(out=y_words[:, HALF:J], in_=y_codes[:, HALF:J].bitcast(I32))
+        for q in range(4):
+            queue = nc.sync if q == 0 else nc.scalar
+            queue.dma_start(out=out_2[0, 4 * q : 4 * q + 4, :].bitcast(I32), in_=y_plane[32 * q : 32 * q + 4, :].bitcast(I32))

@@ -43,54 +43,59 @@ def tile_list_lagged_taps_pl_kernel(tc, xt, w_words, w_scales, cx_words, cx_scal
         cx_plane = sb.tile([P, J], U8, name="cx_plane", align_bytes=64)
         taps = [sb.tile([P, PACK], F32, name=f"tap{i}") for i in range(3)]
 
-        nc.gpsimd.memset(ws_raw[:].rearrange("p g n -> p (g n)").bitcast(I32), 0)
         nc.gpsimd.memset(wcs_raw[:].bitcast(I32), 0)
+        nc.gpsimd.memset(ws_raw[:].rearrange("p g n -> p (g n)").bitcast(I32), 0)
         nc.gpsimd.memset(cx_plane[:].bitcast(I32), 0)
 
         def load_plane(i):
             nc.sync.dma_start(out=planes[i][:], in_=xt_planes[i // PACK, i % PACK])
 
-        def load_scales(tile, scales, quadrants):
+        def load_scales(queue, tile, scales, quadrants):
             for q in quadrants:
-                nc.sync.dma_start(out=tile[32 * q : 32 * q + 4].bitcast(I32), in_=scales[4 * q : 4 * q + 4].bitcast(I32))
+                queue.dma_start(out=tile[32 * q : 32 * q + 4].bitcast(I32), in_=scales[4 * q : 4 * q + 4].bitcast(I32))
 
+        load_scales(nc.gpsimd, cx_plane, cx_scales[0], range(4))
+        load_plane(0)
         nc.sync.dma_start(offsets[:], offs)
-        for tap_tile, tap in zip(taps, (ta, tb, td)):
-            nc.sync.dma_start(out=tap_tile[:], in_=tap.rearrange("(p t) o -> p (t o)", t=PACK))
         nc.sync.dma_start(out=wc_raw[:].bitcast(I32), in_=wc_words[0].bitcast(I32))
         nc.sync.dma_start(out=w_raw[:].bitcast(I32), in_=w_words.rearrange("g p b -> p g b").bitcast(I32))
-        load_plane(0)
-        scale_loads = [(ws_raw, w_scales.rearrange("g r n -> r g n")), (wcs_raw, wc_scales[0]), (cx_plane, cx_scales[0])]
-        for i in range(1, 7):
-            load_plane(i)
-            tile, scales = scale_loads[(i - 1) // 2]
-            load_scales(tile, scales, (0, 1) if i % 2 else (2, 3))
-        load_plane(7)
+        load_plane(1)
         nc.sync.dma_start(out=cx_codes[:].bitcast(I32), in_=cx_words[0].rearrange("p c r -> p (c r)").bitcast(I32))
+        scale_loads = [(wcs_raw, wc_scales[0]), (ws_raw, w_scales.rearrange("g r n -> r g n"))]
+        for i in range(2, 6):
+            load_plane(i)
+            tile, scales = scale_loads[(i - 2) // 2]
+            load_scales(nc.sync, tile, scales, (2, 3) if i % 2 else (0, 1))
+        for tap_tile, tap in zip(taps, (ta, tb, td)):
+            nc.sync.dma_start(out=tap_tile[:], in_=tap.rearrange("(p t) o -> p (t o)", t=PACK))
+        load_plane(6)
+        load_plane(7)
 
         w_codes = sb.tile([P, PASSES, PACK, P], U16, name="w_codes", align_bytes=64)
         wc_codes = sb.tile([P, PACK, P], U16, name="wc_codes", align_bytes=64)
         w_plane = sb.tile([P, PASSES, PACK, P], U8, name="w_plane", align_bytes=64)
         wc_plane = sb.tile([P, PACK, P], U8, name="wc_plane", align_bytes=64)
 
-        picked0 = sb.tile([P, PACK, J], BF16, name="picked0")
+        picked = [sb.tile([P, PACK, J], BF16, name=f"picked{g}") for g in range(PASSES)]
         woven = [sb.tile([P, J, PACK], BF16, name=f"woven{g}", align_bytes=64) for g in range(PASSES)]
         x_codes = [sb.tile([P, J], U32, name=f"x_codes{g}", align_bytes=64) for g in range(PASSES)]
         x_plane = [sb.tile([P, J], U8, name=f"x_plane{g}", align_bytes=64) for g in range(PASSES)]
 
-        def gather0(t):
-            nc.vector.tensor_copy(picked0[:, t, :], planes[t][:].indirect(offsets[:]))
+        def gather(g, t, j0, j1):
+            nc.vector.tensor_copy(picked[g][:, t, j0:j1], planes[PACK * g + t][:].indirect(offsets[:, j0 // 16 : j1 // 16]))
 
+        def weave(engine_copy, dst, src, j0, j1):
+            engine_copy(dst[:, j0:j1, :].rearrange("p (c i) t -> p c t i", i=4), src[:, :, j0:j1].rearrange("p t (c i) -> p c t i", i=4))
+
+        gather(0, 0, 0, J)
+        gather(0, 1, 0, J)
         nc.vector.tensor_copy(wc_codes[:], wc_raw[:].rearrange("p (m t) -> p t m", t=PACK))
-        nc.vector.tensor_copy(w_codes[:], w_raw[:].rearrange("p g (m t) -> p g t m", t=PACK))
-        gather0(0)
-        gather0(1)
+        gather(0, 2, 0, J)
         for g in range(PASSES):
-            nc.vector.tensor_copy(w_plane[:, g], ws_raw[:, g].rearrange("p (m t) -> p t m", t=PACK))
-        gather0(2)
-        gather0(3)
+            nc.vector.tensor_copy(w_codes[:, g], w_raw[:, g].rearrange("p (m t) -> p t m", t=PACK))
+        gather(0, 3, 0, J)
         nc.vector.tensor_copy(wc_plane[:], wcs_raw[:].rearrange("p (m t) -> p t m", t=PACK))
-        nc.scalar.copy(woven[0][:].rearrange("p (c i) t -> p c t i", i=4), picked0[:].rearrange("p t (c i) -> p c t i", i=4))
+        weave(nc.scalar.copy, woven[0], picked[0], 0, J)
 
         acc = sb.tile([P, PACK, J], F32, name="acc")
 
@@ -118,22 +123,29 @@ def tile_list_lagged_taps_pl_kernel(tc, xt, w_words, w_scales, cx_words, cx_scal
                         stop=(g == PASSES - 1 and e == 1 and c == HALF // NMM - 1),
                     )
 
-        nc.vector.tensor_copy(woven[1][:, :, 0], planes[PACK][:].indirect(offsets[:]))
+        for t in range(PACK):
+            context_rows(t)
+        gather(1, 0, 0, J)
         quantize_x(0, 0, J)
+        gather(1, 1, 0, J)
+        for g in range(PASSES):
+            nc.vector.tensor_copy(w_plane[:, g], ws_raw[:, g].rearrange("p (m t) -> p t m", t=PACK))
         for h in range(2):
             for u in range(2):
                 z_pass(0, h, u)
-        for t in range(1, PACK - 1):
-            nc.vector.tensor_copy(woven[1][:, :, t], planes[PACK + t][:].indirect(offsets[:]))
-        for h in range(2):
-            j0 = h * HALF
-            nc.vector.tensor_copy(woven[1][:, j0 : j0 + HALF, PACK - 1], planes[2 * PACK - 1][:].indirect(offsets[:, j0 // 16 : (j0 + HALF) // 16]))
-            quantize_x(1, j0, HALF)
-
+        gather(1, 2, 0, J)
+        gather(1, 3, 0, QUARTER)
+        gather(1, 3, QUARTER, HALF)
+        weave(nc.vector.tensor_copy, woven[1], picked[1], 0, QUARTER)
+        weave(nc.scalar.copy, woven[1], picked[1], QUARTER, HALF)
+        gather(1, 3, HALF, HALF + QUARTER)
+        weave(nc.scalar.copy, woven[1], picked[1], HALF, HALF + QUARTER)
+        gather(1, 3, HALF + QUARTER, J)
+        quantize_x(1, 0, HALF)
+        weave(nc.vector.tensor_copy, woven[1], picked[1], HALF + QUARTER, J)
         for u in range(2):
-            context_rows(2 * u)
-            context_rows(2 * u + 1)
             z_pass(1, 0, u)
+        quantize_x(1, HALF, HALF)
         for u in range(2):
             z_pass(1, 1, u)
 
@@ -142,9 +154,6 @@ def tile_list_lagged_taps_pl_kernel(tc, xt, w_words, w_scales, cx_words, cx_scal
         y_plane = sb.tile([P, J], U8, name="y_plane", align_bytes=64)
         y_rows = out_0.rearrange("(p t) j -> p t j", t=PACK)
         y_words = out_1[0].rearrange("p c r -> p (c r)").bitcast(I32)
-
-        def weave_y(engine_copy, j0, j1):
-            engine_copy(y_woven[:, j0:j1, :].rearrange("p (c i) t -> p c t i", i=4), acc[:, :, j0:j1].rearrange("p t (c i) -> p c t i", i=4))
 
         def quantize_y(j0, width):
             nc.vector.quantize_mx(out=y_codes[:, j0 : j0 + width].bitcast(FP8X4), scales=y_plane[:, j0 : j0 + width], in_=y_woven[:, j0 : j0 + width, :].rearrange("p c t -> p (c t)"))
@@ -164,17 +173,17 @@ def tile_list_lagged_taps_pl_kernel(tc, xt, w_words, w_scales, cx_words, cx_scal
         for u in range(2):
             add_taps(0, u, 0, HALF)
             store_y(0, u)
-        weave_y(nc.scalar.copy, 0, HALF)
+        weave(nc.scalar.copy, y_woven, acc, 0, HALF)
         add_taps(1, 0, 0, HALF)
         store_y(1, 0)
         quantize_y(0, HALF)
         nc.sync.dma_start(out=y_words[:, 0:HALF], in_=y_codes[:, 0:HALF].bitcast(I32))
         add_taps(1, 1, 0, QUARTER)
-        weave_y(nc.scalar.copy, HALF, HALF + QUARTER)
+        weave(nc.scalar.copy, y_woven, acc, HALF, HALF + QUARTER)
         add_taps(1, 1, QUARTER, HALF)
         store_y(1, 1)
-        weave_y(nc.vector.tensor_copy, HALF + QUARTER, HALF + QUARTER + VEC_COLS)
-        weave_y(nc.scalar.copy, HALF + QUARTER + VEC_COLS, J)
+        weave(nc.vector.tensor_copy, y_woven, acc, HALF + QUARTER, HALF + QUARTER + VEC_COLS)
+        weave(nc.scalar.copy, y_woven, acc, HALF + QUARTER + VEC_COLS, J)
         quantize_y(HALF, QUARTER)
         quantize_y(HALF + QUARTER, QUARTER)
         nc.sync.dma_start(out=y_words[:, HALF:J], in_=y_codes[:, HALF:J].bitcast(I32))

@@ -15,14 +15,15 @@ FP8X4 = mybir.dt.float8_e4m3fn_x4
 FP4X4 = mybir.dt.float4_e2m1fn_x4
 MULT = mybir.AluOpType.mult
 ADD = mybir.AluOpType.add
+COPY = mybir.ActivationFunctionType.Copy
 
 P = 128
 PACK = 4
 PASSES = K // (P * PACK)
 HALF = J // 2
 NMM = 128
-QUARTER = J // 4
-VEC_COLS = 80
+VEC_COLS = 160
+SHARED = ((0, 2), (0, 3), (1, 0), (1, 1), (1, 2))
 
 
 def tile_list_lagged_taps_pl_kernel(tc, xt, w_words, w_scales, cx_words, cx_scales, wc_words, wc_scales, ta, tb, td, offs, out_0, out_1, out_2):
@@ -66,88 +67,78 @@ def tile_list_lagged_taps_pl_kernel(tc, xt, w_words, w_scales, cx_words, cx_scal
             load_plane(i)
             tile, scales = scale_loads[(i - 2) // 2]
             load_scales(nc.sync, tile, scales, (2, 3) if i % 2 else (0, 1))
-        for tap_tile, tap in zip(taps, (ta, tb, td)):
-            nc.sync.dma_start(out=tap_tile[:], in_=tap.rearrange("(p t) o -> p (t o)", t=PACK))
         load_plane(6)
         load_plane(7)
+        for tap_tile, tap in zip(taps, (ta, tb, td)):
+            nc.sync.dma_start(out=tap_tile[:], in_=tap.rearrange("(p t) o -> p (t o)", t=PACK))
 
         w_codes = sb.tile([P, PASSES, PACK, P], U16, name="w_codes", align_bytes=64)
         wc_codes = sb.tile([P, PACK, P], U16, name="wc_codes", align_bytes=64)
         w_plane = sb.tile([P, PASSES, PACK, P], U8, name="w_plane", align_bytes=64)
         wc_plane = sb.tile([P, PACK, P], U8, name="wc_plane", align_bytes=64)
 
-        picked = [sb.tile([P, PACK, J], BF16, name=f"picked{g}") for g in range(PASSES)]
+        picked = sb.tile([P, PACK, J], BF16, name="picked")
         woven = [sb.tile([P, J, PACK], BF16, name=f"woven{g}", align_bytes=64) for g in range(PASSES)]
         x_codes = [sb.tile([P, J], U32, name=f"x_codes{g}", align_bytes=64) for g in range(PASSES)]
         x_plane = [sb.tile([P, J], U8, name=f"x_plane{g}", align_bytes=64) for g in range(PASSES)]
 
-        def gather(g, t, j0, j1):
-            nc.vector.tensor_copy(picked[g][:, t, j0:j1], planes[PACK * g + t][:].indirect(offsets[:, j0 // 16 : j1 // 16]))
+        def gather(out, plane, j0, j1):
+            nc.vector.tensor_copy(out, planes[plane][:].indirect(offsets[:, j0 // 16 : j1 // 16]))
 
         def weave(engine_copy, dst, src, j0, j1):
             engine_copy(dst[:, j0:j1, :].rearrange("p (c i) t -> p c t i", i=4), src[:, :, j0:j1].rearrange("p t (c i) -> p c t i", i=4))
 
-        gather(0, 0, 0, J)
-        gather(0, 1, 0, J)
+        gather(picked[:, 0, :], 0, 0, J)
+        gather(picked[:, 1, :], 1, 0, J)
         nc.vector.tensor_copy(wc_codes[:], wc_raw[:].rearrange("p (m t) -> p t m", t=PACK))
-        gather(0, 2, 0, J)
+        gather(picked[:, 2, :], 2, 0, J)
         for g in range(PASSES):
             nc.vector.tensor_copy(w_codes[:, g], w_raw[:, g].rearrange("p (m t) -> p t m", t=PACK))
-        gather(0, 3, 0, J)
+        gather(picked[:, 3, :], 3, 0, J)
         nc.vector.tensor_copy(wc_plane[:], wcs_raw[:].rearrange("p (m t) -> p t m", t=PACK))
-        weave(nc.scalar.copy, woven[0], picked[0], 0, J)
+        weave(nc.scalar.copy, woven[0], picked, 0, J)
 
         acc = sb.tile([P, PACK, J], F32, name="acc")
 
         def context_rows(t):
-            s_bank = ps.tile([P, J], F32, name=f"s_bank{t}")
+            s_bank = ps.tile([P, J], F32, name=f"s_bank{t}", tag=f"bank{PACK + t}")
             nc.tensor.matmul_mx(out=s_bank[:], lhsT=wc_codes[:, t, :].bitcast(FP4X4), lhsT_scale=wc_plane[:, t, :], rhs=cx_codes[:].bitcast(FP8X4), rhs_scale=cx_plane[:], start=True, stop=True)
-            nc.scalar.copy(acc[:, t, :], s_bank[:])
+            nc.scalar.activation(acc[:, t, :], s_bank[:], COPY)
 
         def quantize_x(g, j0, width):
             nc.vector.quantize_mx(out=x_codes[g][:, j0 : j0 + width].bitcast(FP8X4), scales=x_plane[g][:, j0 : j0 + width], in_=woven[g][:, j0 : j0 + width, :].rearrange("p c t -> p (c t)"))
 
-        z_banks = [[ps.tile([P, 2, HALF], F32, name=f"z_bank{h}{u}") for u in range(2)] for h in range(2)]
-
-        def z_pass(g, h, u):
-            for e in range(2):
-                for c in range(HALF // NMM):
-                    j0 = h * HALF + c * NMM
-                    nc.tensor.matmul_mx(
-                        out=z_banks[h][u][:, e, c * NMM : (c + 1) * NMM],
-                        lhsT=w_codes[:, g, 2 * u + e, :].bitcast(FP4X4),
-                        lhsT_scale=w_plane[:, g, 2 * u + e, :],
-                        rhs=x_codes[g][:, j0 : j0 + NMM].bitcast(FP8X4),
-                        rhs_scale=x_plane[g][:, j0 : j0 + NMM],
-                        start=(g == 0 and e == 0 and c == 0),
-                        stop=(g == PASSES - 1 and e == 1 and c == HALF // NMM - 1),
-                    )
+        def z_pass(g, h, t):
+            for c in range(HALF // NMM):
+                j0 = h * HALF + c * NMM
+                nc.tensor.matmul_mx(
+                    out=z_banks[h][t][:, c * NMM : (c + 1) * NMM],
+                    lhsT=w_codes[:, g, t, :].bitcast(FP4X4),
+                    lhsT_scale=w_plane[:, g, t, :],
+                    rhs=x_codes[g][:, j0 : j0 + NMM].bitcast(FP8X4),
+                    rhs_scale=x_plane[g][:, j0 : j0 + NMM],
+                    start=(g == 0 and c == 0),
+                    stop=(g == PASSES - 1 and c == HALF // NMM - 1),
+                )
 
         for t in range(PACK):
             context_rows(t)
-        gather(1, 0, 0, J)
+        z_banks = [[ps.tile([P, HALF], F32, name=f"z_bank{h}{t}", tag=f"bank{PACK * h + t}") for t in range(PACK)] for h in range(2)]
+        gather(woven[1][:, :, 0], PACK + 0, 0, J)
         quantize_x(0, 0, J)
-        gather(1, 1, 0, J)
+        gather(woven[1][:, :, 1], PACK + 1, 0, J)
         for g in range(PASSES):
             nc.vector.tensor_copy(w_plane[:, g], ws_raw[:, g].rearrange("p (m t) -> p t m", t=PACK))
         for h in range(2):
-            for u in range(2):
-                z_pass(0, h, u)
-        gather(1, 2, 0, J)
-        gather(1, 3, 0, QUARTER)
-        gather(1, 3, QUARTER, HALF)
-        weave(nc.vector.tensor_copy, woven[1], picked[1], 0, QUARTER)
-        weave(nc.scalar.copy, woven[1], picked[1], QUARTER, HALF)
-        gather(1, 3, HALF, HALF + QUARTER)
-        weave(nc.scalar.copy, woven[1], picked[1], HALF, HALF + QUARTER)
-        gather(1, 3, HALF + QUARTER, J)
-        quantize_x(1, 0, HALF)
-        weave(nc.vector.tensor_copy, woven[1], picked[1], HALF + QUARTER, J)
-        for u in range(2):
-            z_pass(1, 0, u)
-        quantize_x(1, HALF, HALF)
-        for u in range(2):
-            z_pass(1, 1, u)
+            for t in range(PACK):
+                z_pass(0, h, t)
+        gather(woven[1][:, :, 2], PACK + 2, 0, J)
+        for h in range(2):
+            j0 = h * HALF
+            gather(woven[1][:, j0 : j0 + HALF, PACK - 1], 2 * PACK - 1, j0, j0 + HALF)
+            quantize_x(1, j0, HALF)
+            for t in range(PACK):
+                z_pass(1, h, t)
 
         y_woven = sb.tile([P, J, PACK], BF16, name="y_woven", align_bytes=64)
         y_codes = sb.tile([P, J], U32, name="y_codes", align_bytes=64)
@@ -158,35 +149,35 @@ def tile_list_lagged_taps_pl_kernel(tc, xt, w_words, w_scales, cx_words, cx_scal
         def quantize_y(j0, width):
             nc.vector.quantize_mx(out=y_codes[:, j0 : j0 + width].bitcast(FP8X4), scales=y_plane[:, j0 : j0 + width], in_=y_woven[:, j0 : j0 + width, :].rearrange("p c t -> p (c t)"))
 
-        def add_taps(h, u, c0, c1):
+        def add_taps(h, u):
+            j0 = h * HALF
+            rows = (2 * u, 2 * u + 1)
+            for t in rows:
+                if (h, t) in SHARED:
+                    own = sb.tile([P, HALF], F32, name=f"own{h}{t}")
+                    nc.scalar.activation(own[:], z_banks[h][t][:], COPY, scale=taps[0][:, t : t + 1])
+                    nc.gpsimd.tensor_tensor(acc[:, t, j0 : j0 + HALF], acc[:, t, j0 : j0 + HALF], own[:], ADD)
+            own_rows = [t for t in rows if (h, t) not in SHARED]
             for lag in (2, 1, 0):
-                first = h * HALF + c0 + lag
-                width = min(c1 - c0, J - first)
-                for e in range(2):
-                    t = 2 * u + e
-                    cols = acc[:, t, first : first + width]
-                    nc.vector.scalar_tensor_tensor(cols, z_banks[h][u][:, e, c0 : c0 + width], taps[lag][:, t : t + 1], cols, MULT, ADD)
+                width = min(HALF, J - j0 - lag)
+                for t in own_rows + [t for t in rows if t not in own_rows and lag > 0]:
+                    cols = acc[:, t, j0 + lag : j0 + lag + width]
+                    nc.vector.scalar_tensor_tensor(cols, z_banks[h][t][:, 0:width], taps[lag][:, t : t + 1], cols, MULT, ADD)
+            nc.sync.dma_start(out=y_rows[:, 2 * u : 2 * u + 2, j0 : j0 + HALF], in_=acc[:, 2 * u : 2 * u + 2, j0 : j0 + HALF])
 
-        def store_y(h, u):
-            nc.sync.dma_start(out=y_rows[:, 2 * u : 2 * u + 2, h * HALF : (h + 1) * HALF], in_=acc[:, 2 * u : 2 * u + 2, h * HALF : (h + 1) * HALF])
+        def hand_on(j0):
+            quantize_y(j0, HALF)
+            nc.sync.dma_start(out=y_words[:, j0 : j0 + HALF], in_=y_codes[:, j0 : j0 + HALF].bitcast(I32))
 
-        for u in range(2):
-            add_taps(0, u, 0, HALF)
-            store_y(0, u)
+        add_taps(0, 0)
+        add_taps(0, 1)
+        add_taps(1, 0)
         weave(nc.scalar.copy, y_woven, acc, 0, HALF)
-        add_taps(1, 0, 0, HALF)
-        store_y(1, 0)
-        quantize_y(0, HALF)
-        nc.sync.dma_start(out=y_words[:, 0:HALF], in_=y_codes[:, 0:HALF].bitcast(I32))
-        add_taps(1, 1, 0, QUARTER)
-        weave(nc.scalar.copy, y_woven, acc, HALF, HALF + QUARTER)
-        add_taps(1, 1, QUARTER, HALF)
-        store_y(1, 1)
-        weave(nc.vector.tensor_copy, y_woven, acc, HALF + QUARTER, HALF + QUARTER + VEC_COLS)
-        weave(nc.scalar.copy, y_woven, acc, HALF + QUARTER + VEC_COLS, J)
-        quantize_y(HALF, QUARTER)
-        quantize_y(HALF + QUARTER, QUARTER)
-        nc.sync.dma_start(out=y_words[:, HALF:J], in_=y_codes[:, HALF:J].bitcast(I32))
+        add_taps(1, 1)
+        hand_on(0)
+        weave(nc.vector.tensor_copy, y_woven, acc, HALF, HALF + VEC_COLS)
+        weave(nc.scalar.copy, y_woven, acc, HALF + VEC_COLS, J)
+        hand_on(HALF)
         for q in range(4):
             queue = nc.sync if q == 0 else nc.scalar
             queue.dma_start(out=out_2[0, 4 * q : 4 * q + 4, :].bitcast(I32), in_=y_plane[32 * q : 32 * q + 4, :].bitcast(I32))

@@ -22,8 +22,7 @@ PACK = 4
 PASSES = K // (P * PACK)
 HALF = J // 2
 NMM = 128
-VEC_COLS = 160
-SHARED = ((0, 2), (0, 3), (1, 0), (1, 1), (1, 2))
+VEC_COLS = 128
 
 
 def tile_list_lagged_taps_pl_kernel(tc, xt, w_words, w_scales, cx_words, cx_scales, wc_words, wc_scales, ta, tb, td, offs, out_0, out_1, out_2):
@@ -64,12 +63,12 @@ def tile_list_lagged_taps_pl_kernel(tc, xt, w_words, w_scales, cx_words, cx_scal
         nc.sync.dma_start(out=cx_codes[:].bitcast(I32), in_=cx_words[0].rearrange("p c r -> p (c r)").bitcast(I32))
         scale_loads = [(wcs_raw, wc_scales[0]), (ws_raw, w_scales.rearrange("g r n -> r g n"))]
         for i in range(2, 6):
-            load_plane(i)
             tile, scales = scale_loads[(i - 2) // 2]
             load_scales(nc.sync, tile, scales, (2, 3) if i % 2 else (0, 1))
+            load_plane(i)
         load_plane(6)
         load_plane(7)
-        for tap_tile, tap in zip(taps, (ta, tb, td)):
+        for tap_tile, tap in zip(reversed(taps), (td, tb, ta)):
             nc.sync.dma_start(out=tap_tile[:], in_=tap.rearrange("(p t) o -> p (t o)", t=PACK))
 
         w_codes = sb.tile([P, PASSES, PACK, P], U16, name="w_codes", align_bytes=64)
@@ -92,10 +91,10 @@ def tile_list_lagged_taps_pl_kernel(tc, xt, w_words, w_scales, cx_words, cx_scal
         gather(picked[:, 1, :], 1, 0, J)
         nc.vector.tensor_copy(wc_codes[:], wc_raw[:].rearrange("p (m t) -> p t m", t=PACK))
         gather(picked[:, 2, :], 2, 0, J)
+        nc.vector.tensor_copy(wc_plane[:], wcs_raw[:].rearrange("p (m t) -> p t m", t=PACK))
         for g in range(PASSES):
             nc.vector.tensor_copy(w_codes[:, g], w_raw[:, g].rearrange("p (m t) -> p t m", t=PACK))
         gather(picked[:, 3, :], 3, 0, J)
-        nc.vector.tensor_copy(wc_plane[:], wcs_raw[:].rearrange("p (m t) -> p t m", t=PACK))
         weave(nc.scalar.copy, woven[0], picked, 0, J)
 
         acc = sb.tile([P, PACK, J], F32, name="acc")
@@ -125,10 +124,10 @@ def tile_list_lagged_taps_pl_kernel(tc, xt, w_words, w_scales, cx_words, cx_scal
             context_rows(t)
         z_banks = [[ps.tile([P, HALF], F32, name=f"z_bank{h}{t}", tag=f"bank{PACK * h + t}") for t in range(PACK)] for h in range(2)]
         gather(woven[1][:, :, 0], PACK + 0, 0, J)
-        quantize_x(0, 0, J)
-        gather(woven[1][:, :, 1], PACK + 1, 0, J)
         for g in range(PASSES):
             nc.vector.tensor_copy(w_plane[:, g], ws_raw[:, g].rearrange("p (m t) -> p t m", t=PACK))
+        quantize_x(0, 0, J)
+        gather(woven[1][:, :, 1], PACK + 1, 0, J)
         for h in range(2):
             for t in range(PACK):
                 z_pass(0, h, t)
@@ -149,31 +148,35 @@ def tile_list_lagged_taps_pl_kernel(tc, xt, w_words, w_scales, cx_words, cx_scal
         def quantize_y(j0, width):
             nc.vector.quantize_mx(out=y_codes[:, j0 : j0 + width].bitcast(FP8X4), scales=y_plane[:, j0 : j0 + width], in_=y_woven[:, j0 : j0 + width, :].rearrange("p c t -> p (c t)"))
 
-        def add_taps(h, u):
+        def add_lagged(h, rows, lags):
             j0 = h * HALF
-            rows = (2 * u, 2 * u + 1)
-            for t in rows:
-                if (h, t) in SHARED:
-                    own = sb.tile([P, HALF], F32, name=f"own{h}{t}")
-                    nc.scalar.activation(own[:], z_banks[h][t][:], COPY, scale=taps[0][:, t : t + 1])
-                    nc.gpsimd.tensor_tensor(acc[:, t, j0 : j0 + HALF], acc[:, t, j0 : j0 + HALF], own[:], ADD)
-            own_rows = [t for t in rows if (h, t) not in SHARED]
-            for lag in (2, 1, 0):
+            for lag in lags:
                 width = min(HALF, J - j0 - lag)
-                for t in own_rows + [t for t in rows if t not in own_rows and lag > 0]:
+                for t in rows:
                     cols = acc[:, t, j0 + lag : j0 + lag + width]
                     nc.vector.scalar_tensor_tensor(cols, z_banks[h][t][:, 0:width], taps[lag][:, t : t + 1], cols, MULT, ADD)
-            nc.sync.dma_start(out=y_rows[:, 2 * u : 2 * u + 2, j0 : j0 + HALF], in_=acc[:, 2 * u : 2 * u + 2, j0 : j0 + HALF])
+
+        def store_y(h, u):
+            nc.sync.dma_start(out=y_rows[:, 2 * u : 2 * u + 2, h * HALF : (h + 1) * HALF], in_=acc[:, 2 * u : 2 * u + 2, h * HALF : (h + 1) * HALF])
 
         def hand_on(j0):
             quantize_y(j0, HALF)
             nc.sync.dma_start(out=y_words[:, j0 : j0 + HALF], in_=y_codes[:, j0 : j0 + HALF].bitcast(I32))
 
-        add_taps(0, 0)
-        add_taps(0, 1)
-        add_taps(1, 0)
+        add_lagged(0, range(PACK), (2, 1, 0))
+        for u in range(2):
+            store_y(0, u)
+        for u in range(2):
+            own = sb.tile([P, 2, HALF], F32, name=f"own{u}")
+            for e in range(2):
+                t = 2 * u + e
+                nc.scalar.activation(own[:, e, :], z_banks[1][t][:], COPY, scale=taps[0][:, t : t + 1])
+            cols = acc[:, 2 * u : 2 * u + 2, HALF:J]
+            nc.gpsimd.tensor_tensor(cols, cols, own[:], ADD)
         weave(nc.scalar.copy, y_woven, acc, 0, HALF)
-        add_taps(1, 1)
+        for u in range(2):
+            add_lagged(1, (2 * u, 2 * u + 1), (2, 1))
+            store_y(1, u)
         hand_on(0)
         weave(nc.vector.tensor_copy, y_woven, acc, HALF, HALF + VEC_COLS)
         weave(nc.scalar.copy, y_woven, acc, HALF + VEC_COLS, J)

@@ -20,9 +20,13 @@ COPY = mybir.ActivationFunctionType.Copy
 P = 128
 PACK = 4
 PASSES = K // (P * PACK)
+QUADRANT = 32
+LIVE = 4
+LIST_ROWS = 16
 HALF = J // 2
-NMM = 128
-VEC_COLS = 128
+MM_COLS = 128
+RUN = 4
+VECTOR_COLS = 128
 
 
 def tile_list_lagged_taps_pl_kernel(tc, xt, w_words, w_scales, cx_words, cx_scales, wc_words, wc_scales, ta, tb, td, offs, out_0, out_1, out_2):
@@ -31,156 +35,147 @@ def tile_list_lagged_taps_pl_kernel(tc, xt, w_words, w_scales, cx_words, cx_scal
         sb = ctx.enter_context(tc.tile_pool(name="sb", bufs=1))
         ps = ctx.enter_context(tc.psum_pool(name="ps", bufs=1))
 
-        offsets = sb.tile([P, J // 16], U16, name="offsets")
-        planes = [sb.tile([P, T], F32, name=f"plane{i}") for i in range(PASSES * PACK)]
-        xt_planes = xt.rearrange("(g p t) c -> g t p c", p=P, t=PACK)
+        offsets = sb.tile([P, J // LIST_ROWS], U16, name="offsets")
+        x_rows = [sb.tile([P, T], F32, name=f"x_rows{i}") for i in range(PASSES * PACK)]
+        xt_rows = xt.rearrange("(g p t) c -> g t p c", p=P, t=PACK)
 
         w_raw = sb.tile([P, PASSES, N], U16, name="w_raw")
         wc_raw = sb.tile([P, N], U16, name="wc_raw")
         cx_codes = sb.tile([P, J], U32, name="cx_codes", align_bytes=64)
-        ws_raw = sb.tile([P, PASSES, N], U8, name="ws_raw")
-        wcs_raw = sb.tile([P, N], U8, name="wcs_raw")
-        cx_plane = sb.tile([P, J], U8, name="cx_plane", align_bytes=64)
-        taps = [sb.tile([P, PACK], F32, name=f"tap{i}") for i in range(3)]
+        w_scale_raw = sb.tile([P, PASSES, N], U8, name="w_scale_raw")
+        wc_scale_raw = sb.tile([P, N], U8, name="wc_scale_raw")
+        cx_scale = sb.tile([P, J], U8, name="cx_scale", align_bytes=64)
+        taps = [sb.tile([P, PACK], F32, name=f"tap{lag}") for lag in range(3)]
 
-        nc.gpsimd.memset(wcs_raw[:].bitcast(I32), 0)
-        nc.gpsimd.memset(ws_raw[:].rearrange("p g n -> p (g n)").bitcast(I32), 0)
-        nc.gpsimd.memset(cx_plane[:].bitcast(I32), 0)
+        nc.gpsimd.memset(wc_scale_raw[:].bitcast(I32), 0)
+        nc.gpsimd.memset(w_scale_raw[:].rearrange("p g n -> p (g n)").bitcast(I32), 0)
+        nc.gpsimd.memset(cx_scale[:].bitcast(I32), 0)
 
-        def load_plane(i):
-            nc.sync.dma_start(out=planes[i][:], in_=xt_planes[i // PACK, i % PACK])
+        def load_x(i):
+            nc.sync.dma_start(out=x_rows[i][:], in_=xt_rows[i // PACK, i % PACK])
 
-        def load_scales(queue, tile, scales, quadrants):
+        def load_scales(queue, tile, rows, quadrants):
             for q in quadrants:
-                queue.dma_start(out=tile[32 * q : 32 * q + 4].bitcast(I32), in_=scales[4 * q : 4 * q + 4].bitcast(I32))
+                queue.dma_start(out=tile[QUADRANT * q : QUADRANT * q + LIVE].bitcast(I32), in_=rows[LIVE * q : LIVE * q + LIVE].bitcast(I32))
 
-        load_scales(nc.gpsimd, cx_plane, cx_scales[0], range(4))
-        load_plane(0)
+        load_scales(nc.gpsimd, cx_scale, cx_scales[0], range(4))
+        load_x(0)
         nc.sync.dma_start(offsets[:], offs)
         nc.sync.dma_start(out=wc_raw[:].bitcast(I32), in_=wc_words[0].bitcast(I32))
         nc.sync.dma_start(out=w_raw[:].bitcast(I32), in_=w_words.rearrange("g p b -> p g b").bitcast(I32))
-        load_plane(1)
+        load_x(1)
         nc.sync.dma_start(out=cx_codes[:].bitcast(I32), in_=cx_words[0].rearrange("p c r -> p (c r)").bitcast(I32))
-        scale_loads = [(wcs_raw, wc_scales[0]), (ws_raw, w_scales.rearrange("g r n -> r g n"))]
-        for i in range(2, 6):
-            tile, scales = scale_loads[(i - 2) // 2]
-            load_scales(nc.sync, tile, scales, (2, 3) if i % 2 else (0, 1))
-            load_plane(i)
-        load_plane(6)
-        load_plane(7)
+        w_scale_rows = w_scales.rearrange("g r n -> r g n")
+        load_scales(nc.sync, wc_scale_raw, wc_scales[0], (0, 1))
+        load_x(2)
+        load_scales(nc.sync, wc_scale_raw, wc_scales[0], (2, 3))
+        load_x(3)
+        load_scales(nc.sync, w_scale_raw, w_scale_rows, (0, 1))
+        load_x(4)
+        load_scales(nc.sync, w_scale_raw, w_scale_rows, (2, 3))
+        for i in range(5, PASSES * PACK):
+            load_x(i)
         for tap_tile, tap in zip(reversed(taps), (td, tb, ta)):
             nc.sync.dma_start(out=tap_tile[:], in_=tap.rearrange("(p t) o -> p (t o)", t=PACK))
 
         w_codes = sb.tile([P, PASSES, PACK, P], U16, name="w_codes", align_bytes=64)
         wc_codes = sb.tile([P, PACK, P], U16, name="wc_codes", align_bytes=64)
-        w_plane = sb.tile([P, PASSES, PACK, P], U8, name="w_plane", align_bytes=64)
-        wc_plane = sb.tile([P, PACK, P], U8, name="wc_plane", align_bytes=64)
-
-        picked = sb.tile([P, PACK, J], BF16, name="picked")
-        woven = [sb.tile([P, J, PACK], BF16, name=f"woven{g}", align_bytes=64) for g in range(PASSES)]
+        w_scale = sb.tile([P, PASSES, PACK, P], U8, name="w_scale", align_bytes=64)
+        wc_scale = sb.tile([P, PACK, P], U8, name="wc_scale", align_bytes=64)
+        x_woven = [sb.tile([P, J, PACK], BF16, name=f"x_woven{g}", align_bytes=64) for g in range(PASSES)]
         x_codes = [sb.tile([P, J], U32, name=f"x_codes{g}", align_bytes=64) for g in range(PASSES)]
-        x_plane = [sb.tile([P, J], U8, name=f"x_plane{g}", align_bytes=64) for g in range(PASSES)]
+        x_scale = [sb.tile([P, J], U8, name=f"x_scale{g}", align_bytes=64) for g in range(PASSES)]
 
-        def gather(out, plane, j0, j1):
-            nc.vector.tensor_copy(out, planes[plane][:].indirect(offsets[:, j0 // 16 : j1 // 16]))
+        def deal(dst, src):
+            nc.vector.tensor_copy(dst, src.rearrange("p (m t) -> p t m", t=PACK))
 
-        def weave(engine_copy, dst, src, j0, j1):
-            engine_copy(dst[:, j0:j1, :].rearrange("p (c i) t -> p c t i", i=4), src[:, :, j0:j1].rearrange("p t (c i) -> p c t i", i=4))
+        def gather(g, t, j0, j1):
+            nc.vector.tensor_copy(x_woven[g][:, j0:j1, t], x_rows[PACK * g + t][:].indirect(offsets[:, j0 // LIST_ROWS : j1 // LIST_ROWS]))
 
-        gather(picked[:, 0, :], 0, 0, J)
-        gather(picked[:, 1, :], 1, 0, J)
-        nc.vector.tensor_copy(wc_codes[:], wc_raw[:].rearrange("p (m t) -> p t m", t=PACK))
-        gather(picked[:, 2, :], 2, 0, J)
-        nc.vector.tensor_copy(wc_plane[:], wcs_raw[:].rearrange("p (m t) -> p t m", t=PACK))
+        def quantize(codes, scale, woven, j0, j1):
+            nc.vector.quantize_mx(out=codes[:, j0:j1].bitcast(FP8X4), scales=scale[:, j0:j1], in_=woven[:, j0:j1, :].rearrange("p c t -> p (c t)"))
+
+        gather(0, 0, 0, J)
+        gather(0, 1, 0, J)
+        deal(wc_codes[:], wc_raw[:])
+        gather(0, 2, 0, J)
+        deal(wc_scale[:], wc_scale_raw[:])
         for g in range(PASSES):
-            nc.vector.tensor_copy(w_codes[:, g], w_raw[:, g].rearrange("p (m t) -> p t m", t=PACK))
-        gather(picked[:, 3, :], 3, 0, J)
-        weave(nc.scalar.copy, woven[0], picked, 0, J)
+            deal(w_codes[:, g], w_raw[:, g])
+        gather(0, 3, 0, J)
+        quantize(x_codes[0], x_scale[0], x_woven[0], 0, J)
 
-        acc = sb.tile([P, PACK, J], F32, name="acc")
-
-        def context_rows(t):
-            s_bank = ps.tile([P, J], F32, name=f"s_bank{t}", tag=f"bank{PACK + t}")
-            nc.tensor.matmul_mx(out=s_bank[:], lhsT=wc_codes[:, t, :].bitcast(FP4X4), lhsT_scale=wc_plane[:, t, :], rhs=cx_codes[:].bitcast(FP8X4), rhs_scale=cx_plane[:], start=True, stop=True)
-            nc.scalar.activation(acc[:, t, :], s_bank[:], COPY)
-
-        def quantize_x(g, j0, width):
-            nc.vector.quantize_mx(out=x_codes[g][:, j0 : j0 + width].bitcast(FP8X4), scales=x_plane[g][:, j0 : j0 + width], in_=woven[g][:, j0 : j0 + width, :].rearrange("p c t -> p (c t)"))
-
-        def z_pass(g, h, t):
-            for c in range(HALF // NMM):
-                j0 = h * HALF + c * NMM
-                nc.tensor.matmul_mx(
-                    out=z_banks[h][t][:, c * NMM : (c + 1) * NMM],
-                    lhsT=w_codes[:, g, t, :].bitcast(FP4X4),
-                    lhsT_scale=w_plane[:, g, t, :],
-                    rhs=x_codes[g][:, j0 : j0 + NMM].bitcast(FP8X4),
-                    rhs_scale=x_plane[g][:, j0 : j0 + NMM],
-                    start=(g == 0 and c == 0),
-                    stop=(g == PASSES - 1 and c == HALF // NMM - 1),
-                )
-
+        y = sb.tile([P, PACK, J], F32, name="y")
         for t in range(PACK):
-            context_rows(t)
+            s_bank = ps.tile([P, J], F32, name=f"s_bank{t}", tag=f"bank{PACK + t}")
+            nc.tensor.matmul_mx(out=s_bank[:], lhsT=wc_codes[:, t, :].bitcast(FP4X4), lhsT_scale=wc_scale[:, t, :], rhs=cx_codes[:].bitcast(FP8X4), rhs_scale=cx_scale[:], start=True, stop=True)
+            nc.scalar.activation(y[:, t, :], s_bank[:], COPY)
+
         z_banks = [[ps.tile([P, HALF], F32, name=f"z_bank{h}{t}", tag=f"bank{PACK * h + t}") for t in range(PACK)] for h in range(2)]
-        gather(woven[1][:, :, 0], PACK + 0, 0, J)
+
+        def z_pass(g, h):
+            ranges = HALF // MM_COLS
+            for t in range(PACK):
+                for c in range(ranges):
+                    j0 = h * HALF + c * MM_COLS
+                    nc.tensor.matmul_mx(
+                        out=z_banks[h][t][:, c * MM_COLS : (c + 1) * MM_COLS],
+                        lhsT=w_codes[:, g, t, :].bitcast(FP4X4),
+                        lhsT_scale=w_scale[:, g, t, :],
+                        rhs=x_codes[g][:, j0 : j0 + MM_COLS].bitcast(FP8X4),
+                        rhs_scale=x_scale[g][:, j0 : j0 + MM_COLS],
+                        start=(g == 0 and c == 0),
+                        stop=(g == PASSES - 1 and c == ranges - 1),
+                    )
+
+        gather(1, 0, 0, J)
         for g in range(PASSES):
-            nc.vector.tensor_copy(w_plane[:, g], ws_raw[:, g].rearrange("p (m t) -> p t m", t=PACK))
-        quantize_x(0, 0, J)
-        gather(woven[1][:, :, 1], PACK + 1, 0, J)
+            deal(w_scale[:, g], w_scale_raw[:, g])
+        gather(1, 1, 0, J)
         for h in range(2):
-            for t in range(PACK):
-                z_pass(0, h, t)
-        gather(woven[1][:, :, 2], PACK + 2, 0, J)
+            z_pass(0, h)
+        gather(1, 2, 0, J)
         for h in range(2):
-            j0 = h * HALF
-            gather(woven[1][:, j0 : j0 + HALF, PACK - 1], 2 * PACK - 1, j0, j0 + HALF)
-            quantize_x(1, j0, HALF)
-            for t in range(PACK):
-                z_pass(1, h, t)
+            gather(1, 3, h * HALF, (h + 1) * HALF)
+            quantize(x_codes[1], x_scale[1], x_woven[1], h * HALF, (h + 1) * HALF)
+            z_pass(1, h)
 
         y_woven = sb.tile([P, J, PACK], BF16, name="y_woven", align_bytes=64)
         y_codes = sb.tile([P, J], U32, name="y_codes", align_bytes=64)
-        y_plane = sb.tile([P, J], U8, name="y_plane", align_bytes=64)
-        y_rows = out_0.rearrange("(p t) j -> p t j", t=PACK)
-        y_words = out_1[0].rearrange("p c r -> p (c r)").bitcast(I32)
+        y_scale = sb.tile([P, J], U8, name="y_scale", align_bytes=64)
+        out_rows = out_0.rearrange("(p t) j -> p t j", t=PACK)
+        out_words = out_1[0].rearrange("p c r -> p (c r)").bitcast(I32)
 
-        def quantize_y(j0, width):
-            nc.vector.quantize_mx(out=y_codes[:, j0 : j0 + width].bitcast(FP8X4), scales=y_plane[:, j0 : j0 + width], in_=y_woven[:, j0 : j0 + width, :].rearrange("p c t -> p (c t)"))
-
-        def add_lagged(h, rows, lags):
+        def add_taps_and_store(h, pair, lags):
             j0 = h * HALF
             for lag in lags:
                 width = min(HALF, J - j0 - lag)
-                for t in rows:
-                    cols = acc[:, t, j0 + lag : j0 + lag + width]
+                for t in (2 * pair, 2 * pair + 1):
+                    cols = y[:, t, j0 + lag : j0 + lag + width]
                     nc.vector.scalar_tensor_tensor(cols, z_banks[h][t][:, 0:width], taps[lag][:, t : t + 1], cols, MULT, ADD)
+            nc.sync.dma_start(out=out_rows[:, 2 * pair : 2 * pair + 2, j0 : j0 + HALF], in_=y[:, 2 * pair : 2 * pair + 2, j0 : j0 + HALF])
 
-        def store_y(h, u):
-            nc.sync.dma_start(out=y_rows[:, 2 * u : 2 * u + 2, h * HALF : (h + 1) * HALF], in_=acc[:, 2 * u : 2 * u + 2, h * HALF : (h + 1) * HALF])
+        def weave_y(engine_copy, j0, j1):
+            engine_copy(y_woven[:, j0:j1, :].rearrange("p (c i) t -> p c t i", i=RUN), y[:, :, j0:j1].rearrange("p t (c i) -> p c t i", i=RUN))
 
-        def hand_on(j0):
-            quantize_y(j0, HALF)
-            nc.sync.dma_start(out=y_words[:, j0 : j0 + HALF], in_=y_codes[:, j0 : j0 + HALF].bitcast(I32))
+        def quantize_y_and_store(h):
+            quantize(y_codes, y_scale, y_woven, h * HALF, (h + 1) * HALF)
+            nc.sync.dma_start(out=out_words[:, h * HALF : (h + 1) * HALF], in_=y_codes[:, h * HALF : (h + 1) * HALF].bitcast(I32))
 
-        add_lagged(0, range(PACK), (2, 1, 0))
-        for u in range(2):
-            store_y(0, u)
-        for u in range(2):
-            own = sb.tile([P, 2, HALF], F32, name=f"own{u}")
-            for e in range(2):
-                t = 2 * u + e
-                nc.scalar.activation(own[:, e, :], z_banks[1][t][:], COPY, scale=taps[0][:, t : t + 1])
-            cols = acc[:, 2 * u : 2 * u + 2, HALF:J]
-            nc.gpsimd.tensor_tensor(cols, cols, own[:], ADD)
-        weave(nc.scalar.copy, y_woven, acc, 0, HALF)
-        for u in range(2):
-            add_lagged(1, (2 * u, 2 * u + 1), (2, 1))
-            store_y(1, u)
-        hand_on(0)
-        weave(nc.vector.tensor_copy, y_woven, acc, HALF, HALF + VEC_COLS)
-        weave(nc.scalar.copy, y_woven, acc, HALF + VEC_COLS, J)
-        hand_on(HALF)
+        for pair in range(2):
+            add_taps_and_store(0, pair, (2, 1, 0))
+        for t in range(PACK):
+            unlagged = sb.tile([P, HALF], F32, name=f"unlagged{t}")
+            nc.scalar.activation(unlagged[:], z_banks[1][t][:], COPY, scale=taps[0][:, t : t + 1])
+            nc.gpsimd.tensor_tensor(y[:, t, HALF:J], y[:, t, HALF:J], unlagged[:], ADD)
+        weave_y(nc.scalar.copy, 0, HALF)
+        for pair in range(2):
+            add_taps_and_store(1, pair, (2, 1))
+        quantize_y_and_store(0)
+        weave_y(nc.vector.tensor_copy, HALF, HALF + VECTOR_COLS)
+        weave_y(nc.scalar.copy, HALF + VECTOR_COLS, J)
+        quantize_y_and_store(1)
+
         for q in range(4):
             queue = nc.sync if q == 0 else nc.scalar
-            queue.dma_start(out=out_2[0, 4 * q : 4 * q + 4, :].bitcast(I32), in_=y_plane[32 * q : 32 * q + 4, :].bitcast(I32))
+            queue.dma_start(out=out_2[0, LIVE * q : LIVE * q + LIVE, :].bitcast(I32), in_=y_scale[QUADRANT * q : QUADRANT * q + LIVE, :].bitcast(I32))

from contextlib import ExitStack

import concourse.mybir as mybir

K, T, J, L, N = 1024, 2048, 512, 512, 512
FLOPS = 2 * K * N * J + 2 * L * N * J

F32 = mybir.dt.float32
BF16 = mybir.dt.bfloat16
I32 = mybir.dt.int32
U32 = mybir.dt.uint32
U16 = mybir.dt.uint16
U8 = mybir.dt.uint8
FP8X4 = mybir.dt.float8_e4m3fn_x4
FP4X4 = mybir.dt.float4_e2m1fn_x4
MULT = mybir.AluOpType.mult
ADD = mybir.AluOpType.add
COPY = mybir.ActivationFunctionType.Copy

P = 128
PACK = 4
PASSES = K // (P * PACK)
QUADRANT = 32
LIVE = 4
LIST_ROWS = 16
HALF = J // 2
MM_COLS = 128
RUN = 4
VECTOR_COLS = 128


def tile_list_lagged_taps_pl_kernel(tc, xt, w_words, w_scales, cx_words, cx_scales, wc_words, wc_scales, ta, tb, td, offs, out_0, out_1, out_2):
    nc = tc.nc
    with ExitStack() as ctx:
        sb = ctx.enter_context(tc.tile_pool(name="sb", bufs=1))
        ps = ctx.enter_context(tc.psum_pool(name="ps", bufs=1))

        offsets = sb.tile([P, J // LIST_ROWS], U16, name="offsets")
        x_rows = [sb.tile([P, T], F32, name=f"x_rows{i}") for i in range(PASSES * PACK)]
        xt_rows = xt.rearrange("(g p t) c -> g t p c", p=P, t=PACK)

        w_raw = sb.tile([P, PASSES, N], U16, name="w_raw")
        wc_raw = sb.tile([P, N], U16, name="wc_raw")
        cx_codes = sb.tile([P, J], U32, name="cx_codes", align_bytes=64)
        w_scale_raw = sb.tile([P, PASSES, N], U8, name="w_scale_raw")
        wc_scale_raw = sb.tile([P, N], U8, name="wc_scale_raw")
        cx_scale = sb.tile([P, J], U8, name="cx_scale", align_bytes=64)
        taps = [sb.tile([P, PACK], F32, name=f"tap{lag}") for lag in range(3)]

        nc.gpsimd.memset(wc_scale_raw[:].bitcast(I32), 0)
        nc.gpsimd.memset(w_scale_raw[:].rearrange("p g n -> p (g n)").bitcast(I32), 0)
        nc.gpsimd.memset(cx_scale[:].bitcast(I32), 0)

        def load_x(i):
            nc.sync.dma_start(out=x_rows[i][:], in_=xt_rows[i // PACK, i % PACK])

        def load_scales(queue, tile, rows, quadrants):
            for q in quadrants:
                queue.dma_start(out=tile[QUADRANT * q : QUADRANT * q + LIVE].bitcast(I32), in_=rows[LIVE * q : LIVE * q + LIVE].bitcast(I32))

        load_scales(nc.gpsimd, cx_scale, cx_scales[0], range(4))
        load_x(0)
        nc.sync.dma_start(offsets[:], offs)
        nc.sync.dma_start(out=wc_raw[:].bitcast(I32), in_=wc_words[0].bitcast(I32))
        nc.sync.dma_start(out=w_raw[:].bitcast(I32), in_=w_words.rearrange("g p b -> p g b").bitcast(I32))
        load_x(1)
        nc.sync.dma_start(out=cx_codes[:].bitcast(I32), in_=cx_words[0].rearrange("p c r -> p (c r)").bitcast(I32))
        w_scale_rows = w_scales.rearrange("g r n -> r g n")
        load_scales(nc.sync, wc_scale_raw, wc_scales[0], (0, 1))
        load_x(2)
        load_scales(nc.sync, wc_scale_raw, wc_scales[0], (2, 3))
        load_x(3)
        load_scales(nc.sync, w_scale_raw, w_scale_rows, (0, 1))
        load_x(4)
        load_scales(nc.sync, w_scale_raw, w_scale_rows, (2, 3))
        for i in range(5, PASSES * PACK):
            load_x(i)
        for tap_tile, tap in zip(reversed(taps), (td, tb, ta)):
            nc.sync.dma_start(out=tap_tile[:], in_=tap.rearrange("(p t) o -> p (t o)", t=PACK))

        w_codes = sb.tile([P, PASSES, PACK, P], U16, name="w_codes", align_bytes=64)
        wc_codes = sb.tile([P, PACK, P], U16, name="wc_codes", align_bytes=64)
        w_scale = sb.tile([P, PASSES, PACK, P], U8, name="w_scale", align_bytes=64)
        wc_scale = sb.tile([P, PACK, P], U8, name="wc_scale", align_bytes=64)
        x_woven = [sb.tile([P, J, PACK], BF16, name=f"x_woven{g}", align_bytes=64) for g in range(PASSES)]
        x_codes = [sb.tile([P, J], U32, name=f"x_codes{g}", align_bytes=64) for g in range(PASSES)]
        x_scale = [sb.tile([P, J], U8, name=f"x_scale{g}", align_bytes=64) for g in range(PASSES)]

        def deal(dst, src):
            nc.vector.tensor_copy(dst, src.rearrange("p (m t) -> p t m", t=PACK))

        def gather(g, t, j0, j1):
            nc.vector.tensor_copy(x_woven[g][:, j0:j1, t], x_rows[PACK * g + t][:].indirect(offsets[:, j0 // LIST_ROWS : j1 // LIST_ROWS]))

        def quantize(codes, scale, woven, j0, j1):
            nc.vector.quantize_mx(out=codes[:, j0:j1].bitcast(FP8X4), scales=scale[:, j0:j1], in_=woven[:, j0:j1, :].rearrange("p c t -> p (c t)"))

        gather(0, 0, 0, J)
        gather(0, 1, 0, J)
        deal(wc_codes[:], wc_raw[:])
        gather(0, 2, 0, J)
        deal(wc_scale[:], wc_scale_raw[:])
        for g in range(PASSES):
            deal(w_codes[:, g], w_raw[:, g])
        gather(0, 3, 0, J)
        quantize(x_codes[0], x_scale[0], x_woven[0], 0, J)

        y = sb.tile([P, PACK, J], F32, name="y")
        for t in range(PACK):
            s_bank = ps.tile([P, J], F32, name=f"s_bank{t}", tag=f"bank{PACK + t}")
            nc.tensor.matmul_mx(out=s_bank[:], lhsT=wc_codes[:, t, :].bitcast(FP4X4), lhsT_scale=wc_scale[:, t, :], rhs=cx_codes[:].bitcast(FP8X4), rhs_scale=cx_scale[:], start=True, stop=True)
            nc.scalar.activation(y[:, t, :], s_bank[:], COPY)

        z_banks = [[ps.tile([P, HALF], F32, name=f"z_bank{h}{t}", tag=f"bank{PACK * h + t}") for t in range(PACK)] for h in range(2)]

        def z_pass(g, h):
            ranges = HALF // MM_COLS
            for t in range(PACK):
                for c in range(ranges):
                    j0 = h * HALF + c * MM_COLS
                    nc.tensor.matmul_mx(
                        out=z_banks[h][t][:, c * MM_COLS : (c + 1) * MM_COLS],
                        lhsT=w_codes[:, g, t, :].bitcast(FP4X4),
                        lhsT_scale=w_scale[:, g, t, :],
                        rhs=x_codes[g][:, j0 : j0 + MM_COLS].bitcast(FP8X4),
                        rhs_scale=x_scale[g][:, j0 : j0 + MM_COLS],
                        start=(g == 0 and c == 0),
                        stop=(g == PASSES - 1 and c == ranges - 1),
                    )

        gather(1, 0, 0, J)
        for g in range(PASSES):
            deal(w_scale[:, g], w_scale_raw[:, g])
        gather(1, 1, 0, J)
        for h in range(2):
            z_pass(0, h)
        gather(1, 2, 0, J)
        for h in range(2):
            gather(1, 3, h * HALF, (h + 1) * HALF)
            quantize(x_codes[1], x_scale[1], x_woven[1], h * HALF, (h + 1) * HALF)
            z_pass(1, h)

        y_woven = sb.tile([P, J, PACK], BF16, name="y_woven", align_bytes=64)
        y_codes = sb.tile([P, J], U32, name="y_codes", align_bytes=64)
        y_scale = sb.tile([P, J], U8, name="y_scale", align_bytes=64)
        out_rows = out_0.rearrange("(p t) j -> p t j", t=PACK)
        out_words = out_1[0].rearrange("p c r -> p (c r)").bitcast(I32)

        def add_taps_and_store(h, pair, lags):
            j0 = h * HALF
            for lag in lags:
                width = min(HALF, J - j0 - lag)
                for t in (2 * pair, 2 * pair + 1):
                    cols = y[:, t, j0 + lag : j0 + lag + width]
                    nc.vector.scalar_tensor_tensor(cols, z_banks[h][t][:, 0:width], taps[lag][:, t : t + 1], cols, MULT, ADD)
            nc.sync.dma_start(out=out_rows[:, 2 * pair : 2 * pair + 2, j0 : j0 + HALF], in_=y[:, 2 * pair : 2 * pair + 2, j0 : j0 + HALF])

        def weave_y(engine_copy, j0, j1):
            engine_copy(y_woven[:, j0:j1, :].rearrange("p (c i) t -> p c t i", i=RUN), y[:, :, j0:j1].rearrange("p t (c i) -> p c t i", i=RUN))

        def quantize_y_and_store(h):
            quantize(y_codes, y_scale, y_woven, h * HALF, (h + 1) * HALF)
            nc.sync.dma_start(out=out_words[:, h * HALF : (h + 1) * HALF], in_=y_codes[:, h * HALF : (h + 1) * HALF].bitcast(I32))

        for pair in range(2):
            add_taps_and_store(0, pair, (2, 1, 0))
        for t in range(PACK):
            unlagged = sb.tile([P, HALF], F32, name=f"unlagged{t}")
            nc.scalar.activation(unlagged[:], z_banks[1][t][:], COPY, scale=taps[0][:, t : t + 1])
            nc.gpsimd.tensor_tensor(y[:, t, HALF:J], y[:, t, HALF:J], unlagged[:], ADD)
        weave_y(nc.scalar.copy, 0, HALF)
        for pair in range(2):
            add_taps_and_store(1, pair, (2, 1))
        quantize_y_and_store(0)
        weave_y(nc.vector.tensor_copy, HALF, HALF + VECTOR_COLS)
        weave_y(nc.scalar.copy, HALF + VECTOR_COLS, J)
        quantize_y_and_store(1)

        for q in range(4):
            queue = nc.sync if q == 0 else nc.scalar
            queue.dma_start(out=out_2[0, LIVE * q : LIVE * q + LIVE, :].bitcast(I32), in_=y_scale[QUADRANT * q : QUADRANT * q + LIVE, :].bitcast(I32))
